import numpy as np
import ml_dtypes


def mxq(x, axis, fmt="e4m3"):
    dtype, down = {"e4m3": (ml_dtypes.float8_e4m3fn, 7), "e5m2": (ml_dtypes.float8_e5m2, 14)}[fmt]
    v = np.moveaxis(np.asarray(x, np.float32).astype(ml_dtypes.bfloat16).astype(np.float64), axis, -1)
    blocks = v.reshape(v.shape[:-1] + (-1, 32))
    amax = np.abs(blocks).max(-1, keepdims=True)
    byte = np.maximum(np.where(amax > 0, np.frexp(amax)[1] - 1 + 127, 0) - down, 1)
    scale = np.exp2(byte - 127.0)
    codes = (blocks / scale).astype(np.float32).astype(dtype).astype(np.float64)
    return np.moveaxis((codes * scale).reshape(v.shape), -1, axis)


WIDE = False


def mx_kscale(k):
    if not WIDE:
        return np.ones(k)
    levels = np.array([10, -10, 5, -5, 0])
    if k % 512:
        return np.exp2(np.random.permutation(np.resize(levels, k // 32))).repeat(32)
    a = np.empty((k // 512, 16))
    for p in range(k // 512):
        a[p, :8] = np.random.permutation(np.resize(levels, 8))
        for g in range(8):
            far = levels[np.abs(levels - a[p, g]) >= 10]
            a[p, g + 8] = far[np.random.randint(len(far))]
    return np.exp2(a.ravel()).repeat(32)


def f64(x):
    return np.asarray(x).astype(np.float64)


def striped8(idx):
    return np.concatenate([v.reshape(-1, 16).T for v in idx]).astype(np.uint16)


def unstriped8(offs):
    return np.stack([offs[16 * g:16 * g + 16].T.reshape(-1) for g in range(8)]).astype(np.int64)


E2M1 = np.array([0.0, 0.5, 1.0, 1.5, 2.0, 3.0, 4.0, 6.0, -0.0, -0.5, -1.0, -1.5, -2.0, -3.0, -4.0, -6.0])


def pack_weight(w, fmt):
    k, n = w.shape
    w = f64(np.asarray(w, np.float32).astype(ml_dtypes.bfloat16)).reshape(k // 32, 32, n)
    amax = np.abs(w).max(1)
    if fmt == "e4m3":
        byte = np.frexp(amax)[1] - 1 + 127 - 7
    else:
        mant, ex = np.frexp(amax / 6.0)
        byte = np.where(mant > 0.5, ex, ex - 1) + 127
    byte = np.clip(np.where(amax > 0, byte, 1), 1, 254)
    scaled = (w * np.exp2(127.0 - byte)[:, None, :]).reshape(k, n).astype(np.float32)
    by_word = np.ascontiguousarray(scaled.reshape(k // 512, 128, 4, n).transpose(0, 1, 3, 2))
    if fmt == "e4m3":
        words = by_word.astype(ml_dtypes.float8_e4m3fn).view(np.uint8)
    else:
        c = by_word.astype(ml_dtypes.float4_e2m1fn).view(np.uint8) & 0xF
        words = (c[..., 0::2] | (c[..., 1::2] << 4)).reshape(k // 512, 128, 2 * n)
    return np.ascontiguousarray(words), np.ascontiguousarray(byte.astype(np.uint8).reshape(k // 512, 16, n))


def unpack_weight(words, scales, fmt):
    g, _, n = scales.shape
    words = np.ascontiguousarray(words).reshape(g, 128, n, -1)
    if fmt == "e4m3":
        vals = words.view(ml_dtypes.float8_e4m3fn).astype(np.float64)
    else:
        nib = np.empty((g, 128, n, 4), np.uint8)
        nib[..., 0::2] = words & 0xF
        nib[..., 1::2] = words >> 4
        vals = E2M1[nib]
    vals = vals * np.repeat(np.exp2(scales.astype(np.float64) - 127.0), 8, axis=1)[..., None]
    return vals.transpose(0, 1, 3, 2).reshape(g * 512, n)


def silu(v):
    return v / (1.0 + np.exp(-np.maximum(v, -700.0)))


K, M, T, S = 512, 512, 2048, 1024


def setup_inputs():
    n = np.random.standard_normal
    s = mx_kscale(K)[:, None]
    w = n((K, M)) / np.sqrt(K) / s
    w4 = pack_weight(w, "e2m1")
    rest = w - unpack_weight(*w4, "e2m1")
    p_r8 = pack_weight(rest, "e4m3")
    return {
        "xT": (n((K, T)) * s).astype(np.float32),
        "w4_words": w4[0],
        "w4_scales": w4[1],
        "r8_words": p_r8[0],
        "r8_scales": p_r8[1],
        "wgt": np.repeat(np.random.uniform(0.5, 2.0, (8, S)), 16, axis=0).astype(np.float32),
        "b": (0.3 * n(512)).astype(np.float32),
        "offs": striped8(np.stack([np.random.permutation(T)[:S] for _ in range(8)])),
    }


def reference(xT, w4_words, w4_scales, r8_words, r8_scales, wgt, b, offs):
    idx = unstriped8(offs)
    group = np.arange(K) % 512 // 64
    xg = f64(wgt)[np.arange(K) // 4 % 128] * f64(xT)[np.arange(K)[:, None], idx[group]]
    xT_ = mxq(xg, 0, "e4m3")
    w4_ = unpack_weight(w4_words, w4_scales, "e2m1")
    r8_ = unpack_weight(r8_words, r8_scales, "e4m3")
    y = w4_.T @ xT_ + r8_.T @ xT_
    return silu(y + f64(b)[:, None])

@@ -1,0 +1,117 @@
+import concourse.mybir as mybir
+
+F32 = mybir.dt.float32
+BF16 = mybir.dt.bfloat16
+I32 = mybir.dt.int32
+U32 = mybir.dt.uint32
+U16 = mybir.dt.uint16
+U8 = mybir.dt.uint8
+FP8X4 = mybir.dt.float8_e4m3fn_x4
+FP4X4 = mybir.dt.float4_e2m1fn_x4
+MULT = mybir.AluOpType.mult
+SILU = mybir.ActivationFunctionType.Silu
+
+K, M, T, S = 512, 512, 2048, 1024
+P = 128
+FLOPS = 2 * 2 * K * M * S
+
+CHUNKS = [(0, 128), (128, 384), (384, 640), (640, 896), (896, 1024)]
+NG = 128
+
+
+def tile_list_heads_silu_kernel(tc, xT, w4_words, w4_scales, r8_words, r8_scales, wgt, b, offs, out):
+    nc = tc.nc
+    planes_in_hbm = xT.rearrange("(p i) t -> p i t", i=4)
+    out_rows = out.rearrange("(m p) j -> p m j", p=P)
+
+    with (
+        tc.tile_pool(name="held", bufs=1) as held,
+        tc.psum_pool(name="psum", bufs=8) as psum,
+    ):
+        lists = held.tile([P, S // 16], U16, name="lists")
+        nc.sync.dma_start(lists[:], offs)
+        planes = [held.tile([P, T], F32, name=f"plane{i}") for i in range(4)]
+        weight = held.tile([P, S], F32, name="weight")
+        nc.sync.dma_start(planes[0][:], planes_in_hbm[:, 0, :])
+        nc.sync.dma_start(weight[:, 0:512], wgt[:, 0:512])
+        nc.sync.dma_start(weight[:, 512:1024], wgt[:, 512:1024])
+        for i in range(1, 4):
+            nc.sync.dma_start(planes[i][:], planes_in_hbm[:, i, :])
+
+        zero = held.tile([P, 1], F32, name="zero")
+        nc.vector.memset(zero[:], 0.0)
+        warm = held.tile([P, 1], F32, name="warm")
+        nc.scalar.activation(out=warm[:], in_=zero[:], func=SILU)
+
+        wscales = held.tile([P, 2, M], U8, name="wscales", align_bytes=64)
+        nc.vector.memset(wscales[:].rearrange("p f n -> p (f n)").bitcast(I32), 0)
+        for f, scales in enumerate((w4_scales, r8_scales)):
+            for q in range(4):
+                nc.gpsimd.dma_start(wscales[32 * q : 32 * q + 4, f, :].bitcast(I32), scales[0, 4 * q : 4 * q + 4, :].bitcast(I32))
+
+        w4 = held.tile([P, 2 * M], U8, name="w4", align_bytes=64)
+        nc.sync.dma_start(w4[:].bitcast(I32), w4_words[0].bitcast(I32))
+        r8 = held.tile([P, 4 * M], U8, name="r8", align_bytes=64)
+        nc.sync.dma_start(r8[:].bitcast(I32), r8_words[0].rearrange("p n i -> p (n i)").bitcast(I32))
+
+        bias = held.tile([P, 4], F32, name="bias")
+        with nc.allow_non_contiguous_dma(reason="512 single elements of the bias"):
+            nc.sync.dma_start(bias[:], b.rearrange("(m p) -> p m", p=P))
+
+        picked = held.tile([P, 4, S], F32, name="picked")
+
+        def gather(i, lo, hi):
+            nc.vector.tensor_tensor(
+                picked[:, i, lo:hi], planes[i][:].indirect(lists[:, lo // 16 : hi // 16]), weight[:, lo:hi], MULT
+            )
+
+        grouped = [held.tile([P, hi - lo, 4], BF16, name=f"grouped{c}", align_bytes=64) for c, (lo, hi) in enumerate(CHUNKS)]
+        codes = [held.tile([P, hi - lo], U32, name=f"codes{c}", align_bytes=64) for c, (lo, hi) in enumerate(CHUNKS)]
+        scales = [held.tile([P, hi - lo], U8, name=f"scales{c}", align_bytes=64) for c, (lo, hi) in enumerate(CHUNKS)]
+
+        def pair(copy, c, i):
+            lo, hi = CHUNKS[c]
+            copy(out=grouped[c][:, :, i : i + 2], in_=picked[:, i : i + 2, lo:hi].rearrange("p i n -> p n i"))
+
+        def quantize(c):
+            nc.vector.quantize_mx(
+                out=codes[c][:].bitcast(FP8X4), scales=scales[c][:], in_=grouped[c][:].rearrange("p n i -> p (n i)")
+            )
+
+        def product(c):
+            lo, hi = CHUNKS[c]
+            for h in range(2):
+                res = held.tile([P, 2, hi - lo], F32, name=f"res{c}_{h}")
+                for mm in range(2):
+                    m = 2 * h + mm
+                    acc = psum.tile([P, hi - lo], F32, name="acc")
+                    for n in range(0, hi - lo, NG):
+                        for f, (words, width, fmt) in enumerate(((w4, 2, FP4X4), (r8, 4, FP8X4))):
+                            nc.tensor.matmul_mx(
+                                out=acc[:, n : n + NG],
+                                lhsT=words[:, width * P * m : width * P * (m + 1)].bitcast(fmt),
+                                lhsT_scale=wscales[:, f, P * m : P * (m + 1)],
+                                rhs=codes[c][:, n : n + NG].bitcast(FP8X4),
+                                rhs_scale=scales[c][:, n : n + NG],
+                                start=(f == 0),
+                                stop=(f == 1),
+                            )
+                    nc.scalar.activation(out=res[:, mm, :], in_=acc[:], func=SILU, bias=bias[:, m : m + 1])
+                nc.sync.dma_start(out_rows[:, 2 * h : 2 * h + 2, lo:hi], res[:])
+
+        for i in range(2):
+            for lo in (0, 512):
+                gather(i, lo, lo + 512)
+        for c in range(len(CHUNKS)):
+            pair(nc.scalar.copy, c, 0)
+        for lo in (0, 512):
+            gather(2, lo, lo + 512)
+
+        last = len(CHUNKS) - 1
+        gather(3, *CHUNKS[0])
+        for c in range(last + 1):
+            if c < last:
+                gather(3, *CHUNKS[c + 1])
+            pair(nc.scalar.copy if c == 0 else nc.vector.tensor_copy, c, 2)
+            quantize(c)
+            product(c)

@@ -16,7 +16,7 @@ P = 128
 FLOPS = 2 * 2 * K * M * S
 
 CHUNKS = [(0, 128), (128, 384), (384, 640), (640, 896), (896, 1024)]
-NG = 128
+GROUPS = [(0, 128), (128, 384), (384, 896), (896, 1024)]
 
 
 def tile_list_heads_silu_kernel(tc, xT, w4_words, w4_scales, r8_words, r8_scales, wgt, b, offs, out):
@@ -28,35 +28,47 @@ def tile_list_heads_silu_kernel(tc, xT, w4_words, w4_scales, r8_words, r8_scales
         tc.tile_pool(name="held", bufs=1) as held,
         tc.psum_pool(name="psum", bufs=8) as psum,
     ):
-        lists = held.tile([P, S // 16], U16, name="lists")
-        nc.sync.dma_start(lists[:], offs)
-        planes = [held.tile([P, T], F32, name=f"plane{i}") for i in range(4)]
-        weight = held.tile([P, S], F32, name="weight")
-        nc.sync.dma_start(planes[0][:], planes_in_hbm[:, 0, :])
-        nc.sync.dma_start(weight[:, 0:512], wgt[:, 0:512])
-        nc.sync.dma_start(weight[:, 512:1024], wgt[:, 512:1024])
-        for i in range(1, 4):
-            nc.sync.dma_start(planes[i][:], planes_in_hbm[:, i, :])
-
+        wscales = [held.tile([P, M], U8, name=f"wscales{f}", align_bytes=64) for f in range(2)]
+        brows = held.tile([P, P], F32, name="brows", align_bytes=64)
         zero = held.tile([P, 1], F32, name="zero")
+        nc.vector.memset(brows[:], 0.0)
+        for f in (1, 0):
+            nc.vector.memset(wscales[f][:].bitcast(I32), 0)
         nc.vector.memset(zero[:], 0.0)
         warm = held.tile([P, 1], F32, name="warm")
         nc.scalar.activation(out=warm[:], in_=zero[:], func=SILU)
 
-        wscales = held.tile([P, 2, M], U8, name="wscales", align_bytes=64)
-        nc.vector.memset(wscales[:].rearrange("p f n -> p (f n)").bitcast(I32), 0)
-        for f, scales in enumerate((w4_scales, r8_scales)):
-            for q in range(4):
-                nc.gpsimd.dma_start(wscales[32 * q : 32 * q + 4, f, :].bitcast(I32), scales[0, 4 * q : 4 * q + 4, :].bitcast(I32))
-
+        lists = held.tile([P, S // 16], U16, name="lists")
+        planes = [held.tile([P, T], F32, name=f"plane{i}") for i in range(4)]
+        weight = held.tile([P, S], F32, name="weight")
         w4 = held.tile([P, 2 * M], U8, name="w4", align_bytes=64)
-        nc.sync.dma_start(w4[:].bitcast(I32), w4_words[0].bitcast(I32))
         r8 = held.tile([P, 4 * M], U8, name="r8", align_bytes=64)
+
+        def load_plane(i):
+            nc.sync.dma_start(planes[i][:], planes_in_hbm[:, i, :])
+
+        def load_scales(f, q):
+            rows = (w4_scales, r8_scales)[f][0, 4 * q : 4 * q + 4, :]
+            nc.sync.dma_start(wscales[f][32 * q : 32 * q + 4, :].bitcast(I32), rows.bitcast(I32))
+
+        nc.sync.dma_start(lists[:], offs)
+        load_plane(0)
+        nc.sync.dma_start(brows[0:128:32, :].rearrange("q (m r) -> q m r", m=4), b.rearrange("(m q r) -> q m r", q=4, r=32))
+        for q in range(3):
+            load_scales(1, q)
+        nc.sync.dma_start(weight[:, 0:512], wgt[:, 0:512])
+        nc.sync.dma_start(weight[:, 512:1024], wgt[:, 512:1024])
+        for i in range(1, 4):
+            load_plane(i)
+        load_scales(1, 3)
+        load_scales(0, 0)
+        load_scales(0, 1)
+        nc.sync.dma_start(w4[:].bitcast(I32), w4_words[0].bitcast(I32))
+        load_scales(0, 2)
+        load_scales(0, 3)
         nc.sync.dma_start(r8[:].bitcast(I32), r8_words[0].rearrange("p n i -> p (n i)").bitcast(I32))
 
-        bias = held.tile([P, 4], F32, name="bias")
-        with nc.allow_non_contiguous_dma(reason="512 single elements of the bias"):
-            nc.sync.dma_start(bias[:], b.rearrange("(m p) -> p m", p=P))
+        bias = held.tile([P, P], F32, name="bias", align_bytes=64)
 
         picked = held.tile([P, 4, S], F32, name="picked")
 
@@ -66,52 +78,63 @@ def tile_list_heads_silu_kernel(tc, xT, w4_words, w4_scales, r8_words, r8_scales
             )
 
         grouped = [held.tile([P, hi - lo, 4], BF16, name=f"grouped{c}", align_bytes=64) for c, (lo, hi) in enumerate(CHUNKS)]
-        codes = [held.tile([P, hi - lo], U32, name=f"codes{c}", align_bytes=64) for c, (lo, hi) in enumerate(CHUNKS)]
-        scales = [held.tile([P, hi - lo], U8, name=f"scales{c}", align_bytes=64) for c, (lo, hi) in enumerate(CHUNKS)]
+        codes = [held.tile([P, hi - lo], U32, name=f"codes{g}", align_bytes=64) for g, (lo, hi) in enumerate(GROUPS)]
+        scales = [held.tile([P, hi - lo], U8, name=f"scales{g}", align_bytes=64) for g, (lo, hi) in enumerate(GROUPS)]
 
         def pair(copy, c, i):
             lo, hi = CHUNKS[c]
             copy(out=grouped[c][:, :, i : i + 2], in_=picked[:, i : i + 2, lo:hi].rearrange("p i n -> p n i"))
 
-        def quantize(c):
+        def quantize(c, g):
+            lo, hi = CHUNKS[c][0] - GROUPS[g][0], CHUNKS[c][1] - GROUPS[g][0]
             nc.vector.quantize_mx(
-                out=codes[c][:].bitcast(FP8X4), scales=scales[c][:], in_=grouped[c][:].rearrange("p n i -> p (n i)")
+                out=codes[g][:, lo:hi].bitcast(FP8X4), scales=scales[g][:, lo:hi], in_=grouped[c][:].rearrange("p n i -> p (n i)")
             )
 
-        def product(c):
-            lo, hi = CHUNKS[c]
-            for h in range(2):
-                res = held.tile([P, 2, hi - lo], F32, name=f"res{c}_{h}")
-                for mm in range(2):
-                    m = 2 * h + mm
-                    acc = psum.tile([P, hi - lo], F32, name="acc")
-                    for n in range(0, hi - lo, NG):
-                        for f, (words, width, fmt) in enumerate(((w4, 2, FP4X4), (r8, 4, FP8X4))):
+        def product(g):
+            lo, hi = GROUPS[g]
+            width = hi - lo
+            step = 512 if width == 512 else 128
+            together = 1 if width == 512 else 2
+            for m0 in range(0, 4, together):
+                res = held.tile([P, together, width], F32, name=f"res{g}_{m0}")
+                for mm in range(together):
+                    m = m0 + mm
+                    acc = psum.tile([P, width], F32, name="acc")
+                    for n in range(0, width, step):
+                        for f, (words, size, fmt) in enumerate(((w4, 2, FP4X4), (r8, 4, FP8X4))):
                             nc.tensor.matmul_mx(
-                                out=acc[:, n : n + NG],
-                                lhsT=words[:, width * P * m : width * P * (m + 1)].bitcast(fmt),
-                                lhsT_scale=wscales[:, f, P * m : P * (m + 1)],
-                                rhs=codes[c][:, n : n + NG].bitcast(FP8X4),
-                                rhs_scale=scales[c][:, n : n + NG],
+                                out=acc[:, n : n + step],
+                                lhsT=words[:, size * P * m : size * P * (m + 1)].bitcast(fmt),
+                                lhsT_scale=wscales[f][:, P * m : P * (m + 1)],
+                                rhs=codes[g][:, n : n + step].bitcast(FP8X4),
+                                rhs_scale=scales[g][:, n : n + step],
                                 start=(f == 0),
                                 stop=(f == 1),
                             )
-                    nc.scalar.activation(out=res[:, mm, :], in_=acc[:], func=SILU, bias=bias[:, m : m + 1])
-                nc.sync.dma_start(out_rows[:, 2 * h : 2 * h + 2, lo:hi], res[:])
+                    nc.scalar.activation(out=res[:, mm, :], in_=acc[:], func=SILU, bias=bias[:, 32 * m : 32 * m + 1])
+                nc.sync.dma_start(out_rows[:, m0 : m0 + together, lo:hi], res[:])
 
         for i in range(2):
             for lo in (0, 512):
                 gather(i, lo, lo + 512)
+        nc.vector.transpose(bias[:], brows[:])
         for c in range(len(CHUNKS)):
             pair(nc.scalar.copy, c, 0)
         for lo in (0, 512):
             gather(2, lo, lo + 512)
 
-        last = len(CHUNKS) - 1
         gather(3, *CHUNKS[0])
-        for c in range(last + 1):
-            if c < last:
-                gather(3, *CHUNKS[c + 1])
-            pair(nc.scalar.copy if c == 0 else nc.vector.tensor_copy, c, 2)
-            quantize(c)
-            product(c)
+        pair(nc.scalar.copy, 0, 2)
+        gather(3, *CHUNKS[1])
+        quantize(0, 0)
+        product(0)
+        for c, g in ((1, 1), (2, 2), (3, 2)):
+            pair(nc.vector.tensor_copy, c, 2)
+            gather(3, *CHUNKS[c + 1])
+            quantize(c, g)
+            if c != 2:
+                product(g)
+        pair(nc.vector.tensor_copy, 4, 2)
+        quantize(4, 3)
+        product(3)

import concourse.mybir as mybir

F32 = mybir.dt.float32
BF16 = mybir.dt.bfloat16
I32 = mybir.dt.int32
U32 = mybir.dt.uint32
U16 = mybir.dt.uint16
U8 = mybir.dt.uint8
FP8X4 = mybir.dt.float8_e4m3fn_x4
FP4X4 = mybir.dt.float4_e2m1fn_x4
MULT = mybir.AluOpType.mult
SILU = mybir.ActivationFunctionType.Silu

K, M, T, S = 512, 512, 2048, 1024
P = 128
FLOPS = 2 * 2 * K * M * S

CHUNKS = [(0, 128), (128, 384), (384, 640), (640, 896), (896, 1024)]
GROUPS = [(0, 128), (128, 384), (384, 896), (896, 1024)]


def tile_list_heads_silu_kernel(tc, xT, w4_words, w4_scales, r8_words, r8_scales, wgt, b, offs, out):
    nc = tc.nc
    planes_in_hbm = xT.rearrange("(p i) t -> p i t", i=4)
    out_rows = out.rearrange("(m p) j -> p m j", p=P)

    with (
        tc.tile_pool(name="held", bufs=1) as held,
        tc.psum_pool(name="psum", bufs=8) as psum,
    ):
        wscales = [held.tile([P, M], U8, name=f"wscales{f}", align_bytes=64) for f in range(2)]
        brows = held.tile([P, P], F32, name="brows", align_bytes=64)
        zero = held.tile([P, 1], F32, name="zero")
        nc.vector.memset(brows[:], 0.0)
        for f in (1, 0):
            nc.vector.memset(wscales[f][:].bitcast(I32), 0)
        nc.vector.memset(zero[:], 0.0)
        warm = held.tile([P, 1], F32, name="warm")
        nc.scalar.activation(out=warm[:], in_=zero[:], func=SILU)

        lists = held.tile([P, S // 16], U16, name="lists")
        planes = [held.tile([P, T], F32, name=f"plane{i}") for i in range(4)]
        weight = held.tile([P, S], F32, name="weight")
        w4 = held.tile([P, 2 * M], U8, name="w4", align_bytes=64)
        r8 = held.tile([P, 4 * M], U8, name="r8", align_bytes=64)

        def load_plane(i):
            nc.sync.dma_start(planes[i][:], planes_in_hbm[:, i, :])

        def load_scales(f, q):
            rows = (w4_scales, r8_scales)[f][0, 4 * q : 4 * q + 4, :]
            nc.sync.dma_start(wscales[f][32 * q : 32 * q + 4, :].bitcast(I32), rows.bitcast(I32))

        nc.sync.dma_start(lists[:], offs)
        load_plane(0)
        nc.sync.dma_start(brows[0:128:32, :].rearrange("q (m r) -> q m r", m=4), b.rearrange("(m q r) -> q m r", q=4, r=32))
        for q in range(3):
            load_scales(1, q)
        nc.sync.dma_start(weight[:, 0:512], wgt[:, 0:512])
        nc.sync.dma_start(weight[:, 512:1024], wgt[:, 512:1024])
        for i in range(1, 4):
            load_plane(i)
        load_scales(1, 3)
        load_scales(0, 0)
        load_scales(0, 1)
        nc.sync.dma_start(w4[:].bitcast(I32), w4_words[0].bitcast(I32))
        load_scales(0, 2)
        load_scales(0, 3)
        nc.sync.dma_start(r8[:].bitcast(I32), r8_words[0].rearrange("p n i -> p (n i)").bitcast(I32))

        bias = held.tile([P, P], F32, name="bias", align_bytes=64)

        picked = held.tile([P, 4, S], F32, name="picked")

        def gather(i, lo, hi):
            nc.vector.tensor_tensor(
                picked[:, i, lo:hi], planes[i][:].indirect(lists[:, lo // 16 : hi // 16]), weight[:, lo:hi], MULT
            )

        grouped = [held.tile([P, hi - lo, 4], BF16, name=f"grouped{c}", align_bytes=64) for c, (lo, hi) in enumerate(CHUNKS)]
        codes = [held.tile([P, hi - lo], U32, name=f"codes{g}", align_bytes=64) for g, (lo, hi) in enumerate(GROUPS)]
        scales = [held.tile([P, hi - lo], U8, name=f"scales{g}", align_bytes=64) for g, (lo, hi) in enumerate(GROUPS)]

        def pair(copy, c, i):
            lo, hi = CHUNKS[c]
            copy(out=grouped[c][:, :, i : i + 2], in_=picked[:, i : i + 2, lo:hi].rearrange("p i n -> p n i"))

        def quantize(c, g):
            lo, hi = CHUNKS[c][0] - GROUPS[g][0], CHUNKS[c][1] - GROUPS[g][0]
            nc.vector.quantize_mx(
                out=codes[g][:, lo:hi].bitcast(FP8X4), scales=scales[g][:, lo:hi], in_=grouped[c][:].rearrange("p n i -> p (n i)")
            )

        def product(g):
            lo, hi = GROUPS[g]
            width = hi - lo
            step = 512 if width == 512 else 128
            together = 1 if width == 512 else 2
            for m0 in range(0, 4, together):
                res = held.tile([P, together, width], F32, name=f"res{g}_{m0}")
                for mm in range(together):
                    m = m0 + mm
                    acc = psum.tile([P, width], F32, name="acc")
                    for n in range(0, width, step):
                        for f, (words, size, fmt) in enumerate(((w4, 2, FP4X4), (r8, 4, FP8X4))):
                            nc.tensor.matmul_mx(
                                out=acc[:, n : n + step],
                                lhsT=words[:, size * P * m : size * P * (m + 1)].bitcast(fmt),
                                lhsT_scale=wscales[f][:, P * m : P * (m + 1)],
                                rhs=codes[g][:, n : n + step].bitcast(FP8X4),
                                rhs_scale=scales[g][:, n : n + step],
                                start=(f == 0),
                                stop=(f == 1),
                            )
                    nc.scalar.activation(out=res[:, mm, :], in_=acc[:], func=SILU, bias=bias[:, 32 * m : 32 * m + 1])
                nc.sync.dma_start(out_rows[:, m0 : m0 + together, lo:hi], res[:])

        for i in range(2):
            for lo in (0, 512):
                gather(i, lo, lo + 512)
        nc.vector.transpose(bias[:], brows[:])
        for c in range(len(CHUNKS)):
            pair(nc.scalar.copy, c, 0)
        for lo in (0, 512):
            gather(2, lo, lo + 512)

        gather(3, *CHUNKS[0])
        pair(nc.scalar.copy, 0, 2)
        gather(3, *CHUNKS[1])
        quantize(0, 0)
        product(0)
        for c, g in ((1, 1), (2, 2), (3, 2)):
            pair(nc.vector.tensor_copy, c, 2)
            gather(3, *CHUNKS[c + 1])
            quantize(c, g)
            if c != 2:
                product(g)
        pair(nc.vector.tensor_copy, 4, 2)
        quantize(4, 3)
        product(3)
